import numpy as np
import ml_dtypes


def mxq(x, axis, fmt="e4m3"):
    dtype, down = {"e4m3": (ml_dtypes.float8_e4m3fn, 7), "e5m2": (ml_dtypes.float8_e5m2, 14)}[fmt]
    v = np.moveaxis(np.asarray(x, np.float32).astype(ml_dtypes.bfloat16).astype(np.float64), axis, -1)
    blocks = v.reshape(v.shape[:-1] + (-1, 32))
    amax = np.abs(blocks).max(-1, keepdims=True)
    byte = np.maximum(np.where(amax > 0, np.frexp(amax)[1] - 1 + 127, 0) - down, 1)
    scale = np.exp2(byte - 127.0)
    codes = (blocks / scale).astype(np.float32).astype(dtype).astype(np.float64)
    return np.moveaxis((codes * scale).reshape(v.shape), -1, axis)


WIDE = False


def mx_kscale(k):
    if not WIDE:
        return np.ones(k)
    levels = np.array([30, -30])
    if k % 512:
        return np.exp2(np.random.permutation(np.resize(levels, k // 32))).repeat(32)
    a = np.empty((k // 512, 16))
    for p in range(k // 512):
        a[p, :8] = np.random.permutation(np.resize(levels, 8))
        for g in range(8):
            far = levels[np.abs(levels - a[p, g]) >= 10]
            a[p, g + 8] = far[np.random.randint(len(far))]
    return np.exp2(a.ravel()).repeat(32)


def f64(x):
    return np.asarray(x).astype(np.float64)


def striped(idx):
    return np.tile(np.asarray(idx).reshape(-1, 16).T, (8, 1)).astype(np.uint16)


def unstriped(offs):
    return offs[:16].T.reshape(-1).astype(np.int64)


T, K, N, J = 1024, 512, 1024, 512


def setup_inputs():
    n = np.random.standard_normal
    idx = np.random.permutation(N)[:J]
    ft = mx_kscale(T)
    return {
        "xt": (n((T, K)) * ft[:, None]).astype(np.float32),
        "g": (n((T, N)) * np.exp(0.5 * n((T, 1))) / ft[:, None]).astype(np.float32),
        "mom": (1.0 * n((K, N))).astype(np.float32),
        "sec": (np.random.uniform(0.2, 2.0, (K, N))).astype(np.float32),
        "offs": striped(idx),
    }


def reference(xt, g, mom, sec, offs):
    idx = unstriped(offs)
    xtq = mxq(f64(xt), 0, "e4m3")
    gidxq = mxq(f64(g)[:, idx], 0, "e5m2")
    w = xtq.T @ gidxq
    y = (0.03 * w + 0.9 * f64(mom)[:, idx]) / (np.sqrt(f64(sec)[:, idx]) + 0.1)
    return y

import math
from contextlib import ExitStack

import concourse.mybir as mybir

T, K, N, J = 1024, 512, 1024, 512
FLOPS = 2 * T * K * J

F32 = mybir.dt.float32
BF16 = mybir.dt.bfloat16
U32 = mybir.dt.uint32
U16 = mybir.dt.uint16
U8 = mybir.dt.uint8
E4M3 = mybir.dt.float8_e4m3fn_x4
E5M2 = mybir.dt.float8_e5m2_x4
ACT = mybir.ActivationFunctionType
ALU = mybir.AluOpType

P = 128
PACK = 4
T_PASS = P * PACK
PASSES = T // T_PASS
K_TILES = K // P
HALF_K = K // 2
HALF_J = J // 2
LIST_COLS = J // 16
SPLIT = 336


def interleave(copy, dst, src):
    copy(
        out=dst.rearrange("p (c i) t -> p c t i", i=4),
        in_=src.rearrange("p t (c i) -> p c t i", i=4),
    )


def tile_list_sparse_scaled_step_kernel(tc, xt, g, mom, sec, offs, out):
    nc = tc.nc

    with ExitStack() as ctx:
        sb = ctx.enter_context(tc.tile_pool(name="sb", bufs=1))
        psum = ctx.enter_context(tc.psum_pool(name="psum", bufs=1))

        offsets = sb.tile([P, LIST_COLS], U16, name="offsets")
        nc.sync.dma_start(offsets[:], offs)

        sec_raw = []
        for r in range(K_TILES):
            tile = sb.tile([P, N], F32, name=f"sec_raw{r}")
            nc.sync.dma_start(out=tile[:], in_=sec[r * P : (r + 1) * P, :])
            sec_raw.append(tile)
        g_raw = {}
        for a in range(PASSES):
            rows = g[a * T_PASS : (a + 1) * T_PASS, :].rearrange("(p i) n -> p i n", i=PACK)
            for h in range(2):
                tile = sb.tile([P, 2, N], F32, name=f"g_raw{a}_{h}")
                nc.sync.dma_start(out=tile[:], in_=rows[:, 2 * h : 2 * h + 2, :])
                g_raw[a, h] = tile
        x_raw = []
        for a in range(PASSES):
            tile = sb.tile([P, PACK, K], F32, name=f"x_raw{a}")
            nc.sync.dma_start(
                out=tile[:], in_=xt[a * T_PASS : (a + 1) * T_PASS, :].rearrange("(p i) k -> p i k", i=PACK)
            )
            x_raw.append(tile)
        mom_raw = []
        for r in range(K_TILES):
            tile = sb.tile([P, N], F32, name=f"mom_raw{r}")
            nc.sync.dma_start(out=tile[:], in_=mom[r * P : (r + 1) * P, :])
            mom_raw.append(tile)

        def gather_vector(dst, window, lst):
            nc.vector.tensor_copy(dst, window.indirect(lst))

        def gather_scalar(dst, window, lst):
            nc.scalar.activation(dst, window.indirect(lst), ACT.Copy)

        log_sec = sb.tile([P, K_TILES, J], F32, name="log_sec")
        for r in range(K_TILES):
            picked = sb.tile([P, J], F32, name=f"sec_picked{r}")
            gather_vector(picked[:], sec_raw[r][:], offsets[:])
            nc.scalar.activation(log_sec[:, r, :], picked[:], ACT.Ln, bias=2.0**-60)
        gain = sb.tile([P, K_TILES, J], F32, name="gain")
        nc.scalar.activation(gain[:], log_sec[:], ACT.Sigmoid, bias=math.log(0.1), scale=-0.5)

        g_codes, g_scales = [], []
        for a in range(PASSES):
            picked = sb.tile([P, PACK, J], F32, name=f"g_picked{a}")
            for i in range(PACK):
                on_scalar = a == 1 and i != 2
                gather = gather_scalar if on_scalar else gather_vector
                gather(picked[:, i, :], g_raw[a, i // 2][:, i % 2, :], offsets[:])
            grouped = sb.tile([P, J, PACK], BF16, name=f"g_grouped{a}", align_bytes=64)
            if a == 0:
                interleave(nc.vector.tensor_copy, grouped[:], picked[:])
            else:
                interleave(nc.vector.tensor_copy, grouped[:, :SPLIT, :], picked[:, :, :SPLIT])
                interleave(nc.scalar.copy, grouped[:, SPLIT:, :], picked[:, :, SPLIT:])
            codes = sb.tile([P, J], U32, name=f"g_codes{a}", align_bytes=64)
            scales = sb.tile([P, J], U8, name=f"g_scales{a}", align_bytes=64)
            nc.vector.quantize_mx(
                out=codes[:].bitcast(E5M2), scales=scales[:], in_=grouped[:].rearrange("p c t -> p (c t)")
            )
            g_codes.append(codes)
            g_scales.append(scales)

        acc = [psum.tile([P, J], F32, name=f"acc{r}") for r in range(K_TILES)]

        def multiply(a, r, codes, scales):
            nc.tensor.matmul_mx(
                out=acc[r][:],
                lhsT=codes.bitcast(E4M3),
                lhsT_scale=scales,
                rhs=g_codes[a][:].bitcast(E5M2),
                rhs_scale=g_scales[a][:],
                start=(a == 0),
                stop=(a == PASSES - 1),
            )

        upper = sb.tile([P, PASSES * HALF_K, PACK], BF16, name="x_upper", align_bytes=64)
        for a in range(PASSES):
            lower = sb.tile([P, HALF_K, PACK], BF16, name=f"x_lower{a}", align_bytes=64)
            interleave(nc.vector.tensor_copy, lower[:], x_raw[a][:, :, :HALF_K])
            interleave(nc.scalar.copy, upper[:, a * HALF_K : (a + 1) * HALF_K, :], x_raw[a][:, :, HALF_K:])
            codes = sb.tile([P, HALF_K], U32, name=f"x_lower_codes{a}", align_bytes=64)
            scales = sb.tile([P, HALF_K], U8, name=f"x_lower_scales{a}", align_bytes=64)
            nc.vector.quantize_mx(
                out=codes[:].bitcast(E4M3), scales=scales[:], in_=lower[:].rearrange("p c t -> p (c t)")
            )
            for m in range(2):
                cols = slice(m * P, (m + 1) * P)
                multiply(a, m, codes[:, cols], scales[:, cols])
        codes = sb.tile([P, PASSES * HALF_K], U32, name="x_upper_codes", align_bytes=64)
        scales = sb.tile([P, PASSES * HALF_K], U8, name="x_upper_scales", align_bytes=64)
        nc.vector.quantize_mx(
            out=codes[:].bitcast(E4M3), scales=scales[:], in_=upper[:].rearrange("p c t -> p (c t)")
        )
        for m in range(2):
            for a in range(PASSES):
                cols = slice(a * HALF_K + m * P, a * HALF_K + (m + 1) * P)
                multiply(a, 2 + m, codes[:, cols], scales[:, cols])

        halves = [slice(h * HALF_J, (h + 1) * HALF_J) for h in range(2)]
        for r in range(K_TILES):
            last = r == K_TILES - 1
            picked = sb.tile([P, J], F32, name=f"mom_picked{r}")
            if last:
                for h, cols in enumerate(halves):
                    gather_scalar(picked[:, cols], mom_raw[r][:], offsets[:, h * LIST_COLS // 2 : (h + 1) * LIST_COLS // 2])
            else:
                gather_scalar(picked[:], mom_raw[r][:], offsets[:])
            mix = sb.tile([P, J], F32, name=f"mix{r}")
            for cols in halves:
                nc.vector.scalar_tensor_tensor(
                    out=mix[:, cols], in0=acc[r][:, cols], scalar=0.03 / 0.9, in1=picked[:, cols], op0=ALU.mult, op1=ALU.add
                )
            result = sb.tile([P, J], F32, name=f"result{r}")
            for cols in halves:
                nc.vector.scalar_tensor_tensor(
                    out=result[:, cols], in0=mix[:, cols], scalar=0.9 / 0.1, in1=gain[:, r, cols],
                    op0=ALU.mult, op1=ALU.mult,
                )
                if last:
                    nc.sync.dma_start(out=out[r * P : (r + 1) * P, cols], in_=result[:, cols])
            if not last:
                nc.sync.dma_start(out=out[r * P : (r + 1) * P, :], in_=result[:])
